import numpy as np
import ml_dtypes


def mxq(x, axis, fmt="e4m3"):
    dtype, down = {"e4m3": (ml_dtypes.float8_e4m3fn, 7), "e5m2": (ml_dtypes.float8_e5m2, 14)}[fmt]
    v = np.moveaxis(np.asarray(x, np.float32).astype(ml_dtypes.bfloat16).astype(np.float64), axis, -1)
    blocks = v.reshape(v.shape[:-1] + (-1, 32))
    amax = np.abs(blocks).max(-1, keepdims=True)
    byte = np.maximum(np.where(amax > 0, np.frexp(amax)[1] - 1 + 127, 0) - down, 1)
    scale = np.exp2(byte - 127.0)
    codes = (blocks / scale).astype(np.float32).astype(dtype).astype(np.float64)
    return np.moveaxis((codes * scale).reshape(v.shape), -1, axis)


WIDE = False


def mx_kscale(k):
    if not WIDE:
        return np.ones(k)
    levels = np.array([30, -30])
    if k % 512:
        return np.exp2(np.random.permutation(np.resize(levels, k // 32))).repeat(32)
    a = np.empty((k // 512, 16))
    for p in range(k // 512):
        a[p, :8] = np.random.permutation(np.resize(levels, 8))
        for g in range(8):
            far = levels[np.abs(levels - a[p, g]) >= 10]
            a[p, g + 8] = far[np.random.randint(len(far))]
    return np.exp2(a.ravel()).repeat(32)


def f64(x):
    return np.asarray(x).astype(np.float64)


def striped(idx):
    return np.tile(np.asarray(idx).reshape(-1, 16).T, (8, 1)).astype(np.uint16)


def unstriped(offs):
    return offs[:16].T.reshape(-1).astype(np.int64)


K, J, N, T, V, C = 256, 1024, 256, 2048, 2048, 128


def setup_inputs():
    n = np.random.standard_normal
    idx = np.random.permutation(T)[:J]
    idx2 = np.random.permutation(T)[:J]
    idx3 = np.random.permutation(V)[:J]
    fj = mx_kscale(J)
    return {
        "xf": (n((K, T))).astype(np.float32),
        "ra": (np.random.uniform(0.5, 1.5, (1, J)) * fj).astype(np.float32),
        "gt": (n((N, V)) * np.exp(0.5 * n((1, V)))).astype(np.float32),
        "rb": (np.random.uniform(0.5, 1.5, (1, J)) / fj).astype(np.float32),
        "pc1": (np.random.uniform(0.02, 0.08, (K, N))).astype(np.float32),
        "old": (0.5 * n((K, N))).astype(np.float32),
        "offs": striped(idx),
        "offs2": striped(idx2),
        "offs3": striped(idx3),
    }


def reference(xf, ra, gt, rb, pc1, old, offs, offs2, offs3):
    idx = unstriped(offs)
    idx2 = unstriped(offs2)
    idx3 = unstriped(offs3)
    us = np.maximum(f64(xf)[:, idx], f64(xf)[:, idx2]) * f64(ra)
    uj = us.T
    gg = f64(gt)[:, idx3]
    c1 = gg.reshape(N, C, J // C).mean(axis=2)
    c2 = np.repeat(c1, J // C, axis=1)
    gs = (gg - c2) * f64(rb)
    gj = gs.T
    ujq = mxq(uj, 0, "e4m3")
    gjq = mxq(gj, 0, "e5m2")
    w = ujq.T @ gjq
    w2 = w * f64(pc1)
    y = f64(old) - w2 + 0.2 * np.mean(w2, axis=1, keepdims=True)
    return y

@@ -1,0 +1,207 @@
+from contextlib import ExitStack
+
+import concourse.mybir as mybir
+from concourse.masks import make_identity
+
+K, J, N, T = 256, 1024, 256, 2048
+P = 128
+PACK = 4
+PASS = P * PACK
+PASSES = J // PASS
+SET = 8
+FLOPS = 2 * K * J * N
+
+F32 = mybir.dt.float32
+BF16 = mybir.dt.bfloat16
+U32 = mybir.dt.uint32
+U16 = mybir.dt.uint16
+U8 = mybir.dt.uint8
+E4M3 = mybir.dt.float8_e4m3fn_x4
+E5M2 = mybir.dt.float8_e5m2_x4
+ALU = mybir.AluOpType
+COPY = mybir.ActivationFunctionType.Copy
+
+
+def tile_list_moment_larger_centred_preconditioned_kernel(tc, xf, ra, gt, rb, pc1, old, offs, offs2, offs3, out):
+    nc = tc.nc
+    with ExitStack() as ctx:
+        held = ctx.enter_context(tc.tile_pool(name="held", bufs=1))
+        turn = ctx.enter_context(tc.psum_pool(name="turn", bufs=6))
+        sums = ctx.enter_context(tc.psum_pool(name="sums", bufs=1))
+
+        list_a = held.tile([P, J // 16], U16, name="list_a")
+        list_b = held.tile([P, J // 16], U16, name="list_b")
+        list_g = held.tile([P, J // 16], U16, name="list_g")
+        x_rows = [held.tile([P, T], F32, name=f"x_rows{h}") for h in range(2)]
+        g_rows = [held.tile([P, T], F32, name=f"g_rows{h}") for h in range(2)]
+        ra_t = held.tile([P, PASSES, 8], F32, name="ra_t")
+        rb_t = held.tile([P, PASSES, 8], F32, name="rb_t")
+        pc_sb = held.tile([P, 2, N], F32, name="pc_sb")
+        old_sb = held.tile([P, 2, N], F32, name="old_sb")
+        ident = held.tile([P, P], F32, name="ident")
+
+        nc.sync.dma_start(x_rows[0][:], xf[0:P, :])
+        nc.sync.dma_start(list_a[:], offs)
+        nc.sync.dma_start(list_b[:], offs2)
+        nc.sync.dma_start(list_g[:], offs3)
+        nc.sync.dma_start(g_rows[0][:], gt[0:P, :])
+        nc.sync.dma_start(ra_t[:, :, 0:PACK], ra[0, :].rearrange("(g p t) -> p g t", p=P, t=PACK))
+        nc.sync.dma_start(g_rows[1][:], gt[P : 2 * P, :])
+        nc.sync.dma_start(x_rows[1][:], xf[P : 2 * P, :])
+        nc.sync.dma_start(rb_t[:, :, 0:PACK], rb[0, :].rearrange("(g p t) -> p g t", p=P, t=PACK))
+        nc.sync.dma_start(pc_sb[:], pc1.rearrange("(h p) n -> p h n", p=P))
+        nc.sync.dma_start(old_sb[:], old.rearrange("(h p) n -> p h n", p=P))
+        nc.vector.memset(ident[:], 0.0)
+        make_identity(nc, ident[:], nomemset=True)
+
+        u_codes = [held.tile([P, K], U32, name=f"u_codes{g}", align_bytes=64) for g in range(PASSES)]
+        u_scales = [held.tile([P, K], U8, name=f"u_scales{g}", align_bytes=64) for g in range(PASSES)]
+        g_codes = [held.tile([P, N], U32, name=f"g_codes{g}", align_bytes=64) for g in range(PASSES)]
+        g_scales = [held.tile([P, N], U8, name=f"g_scales{g}", align_bytes=64) for g in range(PASSES)]
+        picked = {}
+
+        def gather(name, rows, offsets, g, on_vector, first=0, size=PASS, tag=""):
+            if name not in picked:
+                picked[name] = held.tile([P, PASS], F32, name=name, tag=tag or name)
+            dense = picked[name]
+            entry = g * PASS + first
+            window = rows[:].indirect(offsets[:, entry // 16 : (entry + size) // 16])
+            if on_vector:
+                nc.vector.tensor_copy(dense[:, first : first + size], window)
+            else:
+                nc.scalar.activation(dense[:, first : first + size], window, COPY)
+
+        def weigh(name, bank, weights, g):
+            woven = held.tile([P, P, PACK], BF16, name=name, align_bytes=64)
+            nc.vector.tensor_tensor(
+                woven[:],
+                bank[:].rearrange("p t c -> p c t"),
+                weights[:, g : g + 1, 0:PACK].to_broadcast([P, P, PACK]),
+                ALU.mult,
+            )
+            picked[name] = woven
+
+        def quantise(name, codes, scales, h, fmt):
+            nc.vector.quantize_mx(
+                out=codes[:, h * P : (h + 1) * P].bitcast(fmt),
+                scales=scales[:, h * P : (h + 1) * P],
+                in_=picked[name][:].rearrange("p c t -> p (c t)"),
+            )
+
+        banks = {}
+
+        def larger(h, g, pieces=1):
+            big = held.tile([P, PACK, P], F32, name=f"big{h}{g}")
+            size = P // pieces
+            for first in range(0, P, size):
+                part = slice(first, first + size)
+                nc.vector.tensor_tensor(
+                    big[:].rearrange("p t q -> p q t")[:, part, :],
+                    picked[f"a{h}{g}"][:].rearrange("p (q t) -> p q t", t=PACK)[:, part, :],
+                    picked[f"b{h}{g}"][:].rearrange("p (q t) -> p q t", t=PACK)[:, part, :],
+                    ALU.max,
+                )
+            bank = turn.tile([P, PACK, P], F32, name="bank")
+            for t in range(PACK):
+                nc.tensor.transpose(bank[:, t, :], big[:, t, :], ident[:])
+            banks[f"u{h}{g}"] = bank
+
+        def centre(h, g):
+            dense = picked[f"g{h}{g}"]
+            total = held.tile([P, PASS // SET, 1], F32, name=f"total{h}{g}")
+            nc.vector.tensor_reduce(
+                total[:, :, 0], dense[:].rearrange("p (c i) -> p c i", i=SET), mybir.AxisListType.X, ALU.add
+            )
+            less = held.tile([P, PASS // SET, 2], F32, name=f"less{h}{g}")
+            nc.gpsimd.tensor_scalar(
+                less[:], total[:].to_broadcast([P, PASS // SET, 2]), -1.0 / SET, 0.0, ALU.mult, ALU.add
+            )
+            bank = turn.tile([P, PACK, P], F32, name="bank")
+            for t in range(PACK):
+                nc.tensor.matmul(
+                    bank[:, t, :], dense[:, t:PASS:PACK], ident[:], start=(t == 0), stop=False, is_transpose=True
+                )
+            for t in range(PACK):
+                nc.tensor.matmul(
+                    bank[:, t, :],
+                    less[:].rearrange("p c s -> p (c s)"),
+                    ident[:],
+                    start=False,
+                    stop=(t == PACK - 1),
+                    is_transpose=True,
+                )
+            banks[f"g{h}{g}"] = bank
+
+        def finish(h):
+            acc = sums.tile([P, N], F32, name=f"acc{h}")
+            cols = slice(h * P, (h + 1) * P)
+            for g in range(PASSES):
+                nc.tensor.matmul_mx(
+                    out=acc[:],
+                    lhsT=u_codes[g][:, cols].bitcast(E4M3),
+                    lhsT_scale=u_scales[g][:, cols],
+                    rhs=g_codes[g][:].bitcast(E5M2),
+                    rhs_scale=g_scales[g][:],
+                    start=(g == 0),
+                    stop=(g == PASSES - 1),
+                )
+            step = held.tile([P, N], F32, name=f"step{h}")
+            row = held.tile([P, 1], F32, name=f"row{h}")
+            nc.vector.scalar_tensor_tensor(step[:], acc[:], -1.0, pc_sb[:, h, :], ALU.mult, ALU.mult, accum_out=row[:])
+            picked[f"step{h}"] = step
+            picked[f"row{h}"] = row
+
+        def store(h):
+            cols = slice(h * P, (h + 1) * P)
+            step = picked[f"step{h}"]
+            row = picked[f"row{h}"]
+            back = held.tile([P, 1], F32, name=f"back{h}")
+            nc.vector.tensor_scalar(back[:], row[:], -0.2 / N, None, ALU.mult)
+            new = held.tile([P, N], F32, name=f"new{h}")
+            nc.vector.scalar_tensor_tensor(new[:], step[:], back[:], old_sb[:, h, :], ALU.add, ALU.add)
+            nc.sync.dma_start(out[cols, :], new[:])
+
+        half = PASS // 2
+        gather("a00", x_rows[0], list_a, 0, False)
+        gather("a01", x_rows[0], list_a, 1, False)
+        gather("g00", g_rows[0], list_g, 0, False)
+        gather("g01", g_rows[0], list_g, 1, False)
+        gather("g10", g_rows[1], list_g, 0, False)
+        gather("g11", g_rows[1], list_g, 1, False, 0, half)
+        gather("a10", x_rows[1], list_a, 0, False)
+        gather("b10", x_rows[1], list_b, 0, False)
+        gather("a11", x_rows[1], list_a, 1, False)
+        gather("b11", x_rows[1], list_b, 1, False, 0, half)
+        gather("b11", x_rows[1], list_b, 1, False, half, half)
+
+        gather("b00", x_rows[0], list_b, 0, True, tag="b0")
+        larger(0, 0)
+        gather("b01", x_rows[0], list_b, 1, True, tag="b0")
+        larger(0, 1)
+        weigh("wu00", banks["u00"], ra_t, 0)
+        centre(0, 0)
+        centre(0, 1)
+        weigh("wu01", banks["u01"], ra_t, 1)
+        gather("g11", g_rows[1], list_g, 1, True, half, half)
+        for g in range(PASSES):
+            quantise(f"wu0{g}", u_codes[g], u_scales[g], 0, E4M3)
+        centre(1, 0)
+        centre(1, 1)
+        weigh("wg00", banks["g00"], rb_t, 0)
+        weigh("wg01", banks["g01"], rb_t, 1)
+        larger(1, 0)
+        weigh("wg10", banks["g10"], rb_t, 0)
+        for g in range(PASSES):
+            quantise(f"wg0{g}", g_codes[g], g_scales[g], 0, E5M2)
+        weigh("wg11", banks["g11"], rb_t, 1)
+        larger(1, 1, pieces=2)
+        for g in range(PASSES):
+            quantise(f"wg1{g}", g_codes[g], g_scales[g], 1, E5M2)
+        weigh("wu10", banks["u10"], ra_t, 0)
+        quantise("wu10", u_codes[0], u_scales[0], 1, E4M3)
+        weigh("wu11", banks["u11"], ra_t, 1)
+        finish(0)
+        quantise("wu11", u_codes[1], u_scales[1], 1, E4M3)
+        store(0)
+        finish(1)
+        store(1)

@@ -45,13 +45,16 @@ def tile_list_moment_larger_centred_preconditioned_kernel(tc, xf, ra, gt, rb, pc
         nc.sync.dma_start(list_b[:], offs2)
         nc.sync.dma_start(list_g[:], offs3)
         nc.sync.dma_start(g_rows[0][:], gt[0:P, :])
+        nc.sync.dma_start(g_rows[1][:, 0 : T // 2], gt[P : 2 * P, 0 : T // 2])
         nc.sync.dma_start(ra_t[:, :, 0:PACK], ra[0, :].rearrange("(g p t) -> p g t", p=P, t=PACK))
-        nc.sync.dma_start(g_rows[1][:], gt[P : 2 * P, :])
+        nc.sync.dma_start(g_rows[1][:, T // 2 : T], gt[P : 2 * P, T // 2 : T])
         nc.sync.dma_start(x_rows[1][:], xf[P : 2 * P, :])
         nc.sync.dma_start(rb_t[:, :, 0:PACK], rb[0, :].rearrange("(g p t) -> p g t", p=P, t=PACK))
         nc.sync.dma_start(pc_sb[:], pc1.rearrange("(h p) n -> p h n", p=P))
         nc.sync.dma_start(old_sb[:], old.rearrange("(h p) n -> p h n", p=P))
         nc.vector.memset(ident[:], 0.0)
+        warm = held.tile([P, 1], F32, name="warm")
+        nc.scalar.activation(warm[:], ident[:, 0:1], COPY)
         make_identity(nc, ident[:], nomemset=True)
 
         u_codes = [held.tile([P, K], U32, name=f"u_codes{g}", align_bytes=64) for g in range(PASSES)]
@@ -60,9 +63,9 @@ def tile_list_moment_larger_centred_preconditioned_kernel(tc, xf, ra, gt, rb, pc
         g_scales = [held.tile([P, N], U8, name=f"g_scales{g}", align_bytes=64) for g in range(PASSES)]
         picked = {}
 
-        def gather(name, rows, offsets, g, on_vector, first=0, size=PASS, tag=""):
+        def gather(name, rows, offsets, g, on_vector, first=0, size=PASS):
             if name not in picked:
-                picked[name] = held.tile([P, PASS], F32, name=name, tag=tag or name)
+                picked[name] = held.tile([P, PASS], F32, name=name)
             dense = picked[name]
             entry = g * PASS + first
             window = rows[:].indirect(offsets[:, entry // 16 : (entry + size) // 16])
@@ -174,12 +177,12 @@ def tile_list_moment_larger_centred_preconditioned_kernel(tc, xf, ra, gt, rb, pc
         gather("b11", x_rows[1], list_b, 1, False, 0, half)
         gather("b11", x_rows[1], list_b, 1, False, half, half)
 
-        gather("b00", x_rows[0], list_b, 0, True, tag="b0")
+        gather("b00", x_rows[0], list_b, 0, True)
+        gather("b01", x_rows[0], list_b, 1, True)
         larger(0, 0)
-        gather("b01", x_rows[0], list_b, 1, True, tag="b0")
         larger(0, 1)
-        weigh("wu00", banks["u00"], ra_t, 0)
         centre(0, 0)
+        weigh("wu00", banks["u00"], ra_t, 0)
         centre(0, 1)
         weigh("wu01", banks["u01"], ra_t, 1)
         gather("g11", g_rows[1], list_g, 1, True, half, half)

@@ -45,9 +45,8 @@ def tile_list_moment_larger_centred_preconditioned_kernel(tc, xf, ra, gt, rb, pc
         nc.sync.dma_start(list_b[:], offs2)
         nc.sync.dma_start(list_g[:], offs3)
         nc.sync.dma_start(g_rows[0][:], gt[0:P, :])
-        nc.sync.dma_start(g_rows[1][:, 0 : T // 2], gt[P : 2 * P, 0 : T // 2])
+        nc.sync.dma_start(g_rows[1][:], gt[P : 2 * P, :])
         nc.sync.dma_start(ra_t[:, :, 0:PACK], ra[0, :].rearrange("(g p t) -> p g t", p=P, t=PACK))
-        nc.sync.dma_start(g_rows[1][:, T // 2 : T], gt[P : 2 * P, T // 2 : T])
         nc.sync.dma_start(x_rows[1][:], xf[P : 2 * P, :])
         nc.sync.dma_start(rb_t[:, :, 0:PACK], rb[0, :].rearrange("(g p t) -> p g t", p=P, t=PACK))
         nc.sync.dma_start(pc_sb[:], pc1.rearrange("(h p) n -> p h n", p=P))
@@ -75,7 +74,7 @@ def tile_list_moment_larger_centred_preconditioned_kernel(tc, xf, ra, gt, rb, pc
                 nc.scalar.activation(dense[:, first : first + size], window, COPY)
 
         def weigh(name, bank, weights, g):
-            woven = held.tile([P, P, PACK], BF16, name=name, align_bytes=64)
+            woven = held.tile([P, P, PACK], BF16, name=name, tag=name, align_bytes=64)
             nc.vector.tensor_tensor(
                 woven[:],
                 bank[:].rearrange("p t c -> p c t"),
@@ -135,22 +134,24 @@ def tile_list_moment_larger_centred_preconditioned_kernel(tc, xf, ra, gt, rb, pc
                 )
             banks[f"g{h}{g}"] = bank
 
-        def finish(h):
-            acc = sums.tile([P, N], F32, name=f"acc{h}")
+        acc = [sums.tile([P, N], F32, name=f"acc{h}") for h in range(2)]
+
+        def multiply(h, g):
             cols = slice(h * P, (h + 1) * P)
-            for g in range(PASSES):
-                nc.tensor.matmul_mx(
-                    out=acc[:],
-                    lhsT=u_codes[g][:, cols].bitcast(E4M3),
-                    lhsT_scale=u_scales[g][:, cols],
-                    rhs=g_codes[g][:].bitcast(E5M2),
-                    rhs_scale=g_scales[g][:],
-                    start=(g == 0),
-                    stop=(g == PASSES - 1),
-                )
-            step = held.tile([P, N], F32, name=f"step{h}")
+            nc.tensor.matmul_mx(
+                out=acc[h][:],
+                lhsT=u_codes[g][:, cols].bitcast(E4M3),
+                lhsT_scale=u_scales[g][:, cols],
+                rhs=g_codes[g][:].bitcast(E5M2),
+                rhs_scale=g_scales[g][:],
+                start=(g == 0),
+                stop=(g == PASSES - 1),
+            )
+
+        def finish(h, tag):
+            step = held.tile([P, N], F32, name=f"step{h}", tag=tag, align_bytes=64)
             row = held.tile([P, 1], F32, name=f"row{h}")
-            nc.vector.scalar_tensor_tensor(step[:], acc[:], -1.0, pc_sb[:, h, :], ALU.mult, ALU.mult, accum_out=row[:])
+            nc.vector.scalar_tensor_tensor(step[:], acc[h][:], -1.0, pc_sb[:, h, :], ALU.mult, ALU.mult, accum_out=row[:])
             picked[f"step{h}"] = step
             picked[f"row{h}"] = row
 
@@ -165,46 +166,48 @@ def tile_list_moment_larger_centred_preconditioned_kernel(tc, xf, ra, gt, rb, pc
             nc.sync.dma_start(out[cols, :], new[:])
 
         half = PASS // 2
+        gather("b00", x_rows[0], list_b, 0, True)
+        gather("b01", x_rows[0], list_b, 1, True)
+        gather("b11", x_rows[1], list_b, 1, True, 0, half)
         gather("a00", x_rows[0], list_a, 0, False)
         gather("a01", x_rows[0], list_a, 1, False)
-        gather("g00", g_rows[0], list_g, 0, False)
-        gather("g01", g_rows[0], list_g, 1, False)
-        gather("g10", g_rows[1], list_g, 0, False)
-        gather("g11", g_rows[1], list_g, 1, False, 0, half)
+        for h in range(2):
+            for g in range(PASSES):
+                gather(f"g{h}{g}", g_rows[h], list_g, g, False)
         gather("a10", x_rows[1], list_a, 0, False)
         gather("b10", x_rows[1], list_b, 0, False)
         gather("a11", x_rows[1], list_a, 1, False)
-        gather("b11", x_rows[1], list_b, 1, False, 0, half)
         gather("b11", x_rows[1], list_b, 1, False, half, half)
 
-        gather("b00", x_rows[0], list_b, 0, True)
-        gather("b01", x_rows[0], list_b, 1, True)
         larger(0, 0)
         larger(0, 1)
         centre(0, 0)
-        weigh("wu00", banks["u00"], ra_t, 0)
         centre(0, 1)
+        weigh("wu00", banks["u00"], ra_t, 0)
         weigh("wu01", banks["u01"], ra_t, 1)
-        gather("g11", g_rows[1], list_g, 1, True, half, half)
+        centre(1, 0)
         for g in range(PASSES):
             quantise(f"wu0{g}", u_codes[g], u_scales[g], 0, E4M3)
-        centre(1, 0)
         centre(1, 1)
         weigh("wg00", banks["g00"], rb_t, 0)
         weigh("wg01", banks["g01"], rb_t, 1)
         larger(1, 0)
-        weigh("wg10", banks["g10"], rb_t, 0)
         for g in range(PASSES):
             quantise(f"wg0{g}", g_codes[g], g_scales[g], 0, E5M2)
-        weigh("wg11", banks["g11"], rb_t, 1)
         larger(1, 1, pieces=2)
+        weigh("wg10", banks["g10"], rb_t, 0)
+        weigh("wg11", banks["g11"], rb_t, 1)
+        weigh("wu10", banks["u10"], ra_t, 0)
         for g in range(PASSES):
             quantise(f"wg1{g}", g_codes[g], g_scales[g], 1, E5M2)
-        weigh("wu10", banks["u10"], ra_t, 0)
         quantise("wu10", u_codes[0], u_scales[0], 1, E4M3)
+        multiply(0, 0)
+        multiply(0, 1)
+        multiply(1, 0)
         weigh("wu11", banks["u11"], ra_t, 1)
-        finish(0)
         quantise("wu11", u_codes[1], u_scales[1], 1, E4M3)
+        multiply(1, 1)
+        finish(0, "wu11")
         store(0)
-        finish(1)
+        finish(1, "step1")
         store(1)

@@ -5,10 +5,15 @@ from concourse.masks import make_identity
 
 K, J, N, T = 256, 1024, 256, 2048
 P = 128
+HALVES = 2
 PACK = 4
 PASS = P * PACK
 PASSES = J // PASS
 SET = 8
+PER_COLUMN = 16
+WEIGHT_ROW = 8
+GRADIENT_ON_SCALAR = 256
+FEATURE_ON_VECTOR = 384
 FLOPS = 2 * K * J * N
 
 F32 = mybir.dt.float32
@@ -29,94 +34,78 @@ def tile_list_moment_larger_centred_preconditioned_kernel(tc, xf, ra, gt, rb, pc
         turn = ctx.enter_context(tc.psum_pool(name="turn", bufs=6))
         sums = ctx.enter_context(tc.psum_pool(name="sums", bufs=1))
 
-        list_a = held.tile([P, J // 16], U16, name="list_a")
-        list_b = held.tile([P, J // 16], U16, name="list_b")
-        list_g = held.tile([P, J // 16], U16, name="list_g")
-        x_rows = [held.tile([P, T], F32, name=f"x_rows{h}") for h in range(2)]
-        g_rows = [held.tile([P, T], F32, name=f"g_rows{h}") for h in range(2)]
-        ra_t = held.tile([P, PASSES, 8], F32, name="ra_t")
-        rb_t = held.tile([P, PASSES, 8], F32, name="rb_t")
-        pc_sb = held.tile([P, 2, N], F32, name="pc_sb")
-        old_sb = held.tile([P, 2, N], F32, name="old_sb")
+        lists = {side: held.tile([P, J // PER_COLUMN], U16, name=f"list_{side}") for side in "abg"}
+        x_rows = [held.tile([P, T], F32, name=f"x_rows{h}") for h in range(HALVES)]
+        g_rows = [held.tile([P, T], F32, name=f"g_rows{h}") for h in range(HALVES)]
+        tables = {"a": x_rows, "b": x_rows, "g": g_rows}
+        weights = {side: held.tile([P, PASSES, WEIGHT_ROW], F32, name=f"weights_{side}") for side in "ug"}
+        pc_sb = held.tile([P, HALVES, N], F32, name="pc_sb")
+        old_sb = held.tile([P, HALVES, N], F32, name="old_sb")
         ident = held.tile([P, P], F32, name="ident")
 
+        by_slot = "(g p t) -> p g t"
         nc.sync.dma_start(x_rows[0][:], xf[0:P, :])
-        nc.sync.dma_start(list_a[:], offs)
-        nc.sync.dma_start(list_b[:], offs2)
-        nc.sync.dma_start(list_g[:], offs3)
+        nc.sync.dma_start(lists["a"][:], offs)
+        nc.sync.dma_start(lists["b"][:], offs2)
+        nc.sync.dma_start(lists["g"][:], offs3)
         nc.sync.dma_start(g_rows[0][:], gt[0:P, :])
         nc.sync.dma_start(g_rows[1][:], gt[P : 2 * P, :])
-        nc.sync.dma_start(ra_t[:, :, 0:PACK], ra[0, :].rearrange("(g p t) -> p g t", p=P, t=PACK))
+        nc.sync.dma_start(weights["u"][:, :, 0:PACK], ra[0, :].rearrange(by_slot, p=P, t=PACK))
         nc.sync.dma_start(x_rows[1][:], xf[P : 2 * P, :])
-        nc.sync.dma_start(rb_t[:, :, 0:PACK], rb[0, :].rearrange("(g p t) -> p g t", p=P, t=PACK))
+        nc.sync.dma_start(weights["g"][:, :, 0:PACK], rb[0, :].rearrange(by_slot, p=P, t=PACK))
         nc.sync.dma_start(pc_sb[:], pc1.rearrange("(h p) n -> p h n", p=P))
         nc.sync.dma_start(old_sb[:], old.rearrange("(h p) n -> p h n", p=P))
+
         nc.vector.memset(ident[:], 0.0)
         warm = held.tile([P, 1], F32, name="warm")
         nc.scalar.activation(warm[:], ident[:, 0:1], COPY)
         make_identity(nc, ident[:], nomemset=True)
 
-        u_codes = [held.tile([P, K], U32, name=f"u_codes{g}", align_bytes=64) for g in range(PASSES)]
-        u_scales = [held.tile([P, K], U8, name=f"u_scales{g}", align_bytes=64) for g in range(PASSES)]
-        g_codes = [held.tile([P, N], U32, name=f"g_codes{g}", align_bytes=64) for g in range(PASSES)]
-        g_scales = [held.tile([P, N], U8, name=f"g_scales{g}", align_bytes=64) for g in range(PASSES)]
-        picked = {}
+        codes, scales = {}, {}
+        for side, width in (("u", K), ("g", N)):
+            for g in range(PASSES):
+                codes[side, g] = held.tile([P, width], U32, name=f"codes_{side}{g}", align_bytes=64)
+            for g in range(PASSES):
+                scales[side, g] = held.tile([P, width], U8, name=f"scales_{side}{g}", align_bytes=64)
+        formats = {"u": E4M3, "g": E5M2}
+        acc = [sums.tile([P, N], F32, name=f"acc{h}") for h in range(HALVES)]
 
-        def gather(name, rows, offsets, g, on_vector, first=0, size=PASS):
-            if name not in picked:
-                picked[name] = held.tile([P, PASS], F32, name=name)
-            dense = picked[name]
-            entry = g * PASS + first
-            window = rows[:].indirect(offsets[:, entry // 16 : (entry + size) // 16])
+        picked, banks, woven = {}, {}, {}
+
+        def gather(side, h, g, on_vector, first=0, end=PASS):
+            if (side, h, g) not in picked:
+                picked[side, h, g] = held.tile([P, PASS], F32, name=f"picked_{side}{h}{g}")
+            columns = slice((g * PASS + first) // PER_COLUMN, (g * PASS + end) // PER_COLUMN)
+            window = tables[side][h][:].indirect(lists[side][:, columns])
             if on_vector:
-                nc.vector.tensor_copy(dense[:, first : first + size], window)
+                nc.vector.tensor_copy(picked[side, h, g][:, first:end], window)
             else:
-                nc.scalar.activation(dense[:, first : first + size], window, COPY)
+                nc.scalar.activation(picked[side, h, g][:, first:end], window, COPY)
 
-        def weigh(name, bank, weights, g):
-            woven = held.tile([P, P, PACK], BF16, name=name, tag=name, align_bytes=64)
-            nc.vector.tensor_tensor(
-                woven[:],
-                bank[:].rearrange("p t c -> p c t"),
-                weights[:, g : g + 1, 0:PACK].to_broadcast([P, P, PACK]),
-                ALU.mult,
-            )
-            picked[name] = woven
-
-        def quantise(name, codes, scales, h, fmt):
-            nc.vector.quantize_mx(
-                out=codes[:, h * P : (h + 1) * P].bitcast(fmt),
-                scales=scales[:, h * P : (h + 1) * P],
-                in_=picked[name][:].rearrange("p c t -> p (c t)"),
-            )
-
-        banks = {}
-
-        def larger(h, g, pieces=1):
+        def larger(h, g, cuts=(0, PASS)):
             big = held.tile([P, PACK, P], F32, name=f"big{h}{g}")
-            size = P // pieces
-            for first in range(0, P, size):
-                part = slice(first, first + size)
+            for first, end in zip(cuts, cuts[1:]):
+                part = slice(first // PACK, end // PACK)
                 nc.vector.tensor_tensor(
                     big[:].rearrange("p t q -> p q t")[:, part, :],
-                    picked[f"a{h}{g}"][:].rearrange("p (q t) -> p q t", t=PACK)[:, part, :],
-                    picked[f"b{h}{g}"][:].rearrange("p (q t) -> p q t", t=PACK)[:, part, :],
+                    picked["a", h, g][:].rearrange("p (q t) -> p q t", t=PACK)[:, part, :],
+                    picked["b", h, g][:].rearrange("p (q t) -> p q t", t=PACK)[:, part, :],
                     ALU.max,
                 )
             bank = turn.tile([P, PACK, P], F32, name="bank")
             for t in range(PACK):
                 nc.tensor.transpose(bank[:, t, :], big[:, t, :], ident[:])
-            banks[f"u{h}{g}"] = bank
+            banks["u", h, g] = bank
 
         def centre(h, g):
-            dense = picked[f"g{h}{g}"]
+            dense = picked["g", h, g]
             total = held.tile([P, PASS // SET, 1], F32, name=f"total{h}{g}")
             nc.vector.tensor_reduce(
                 total[:, :, 0], dense[:].rearrange("p (c i) -> p c i", i=SET), mybir.AxisListType.X, ALU.add
             )
-            less = held.tile([P, PASS // SET, 2], F32, name=f"less{h}{g}")
+            less = held.tile([P, PASS // SET, SET // PACK], F32, name=f"less{h}{g}")
             nc.gpsimd.tensor_scalar(
-                less[:], total[:].to_broadcast([P, PASS // SET, 2]), -1.0 / SET, 0.0, ALU.mult, ALU.add
+                less[:], total[:].to_broadcast([P, PASS // SET, SET // PACK]), -1.0 / SET, 0.0, ALU.mult, ALU.add
             )
             bank = turn.tile([P, PACK, P], F32, name="bank")
             for t in range(PACK):
@@ -132,18 +121,35 @@ def tile_list_moment_larger_centred_preconditioned_kernel(tc, xf, ra, gt, rb, pc
                     stop=(t == PACK - 1),
                     is_transpose=True,
                 )
-            banks[f"g{h}{g}"] = bank
+            banks["g", h, g] = bank
 
-        acc = [sums.tile([P, N], F32, name=f"acc{h}") for h in range(2)]
+        def weigh(side, h, g):
+            woven[side, h, g] = held.tile(
+                [P, P, PACK], BF16, name=f"woven_{side}{h}{g}", tag=f"woven_{side}{h}{g}", align_bytes=64
+            )
+            nc.vector.tensor_tensor(
+                woven[side, h, g][:],
+                banks[side, h, g][:].rearrange("p t c -> p c t"),
+                weights[side][:, g : g + 1, 0:PACK].to_broadcast([P, P, PACK]),
+                ALU.mult,
+            )
+
+        def quantise(side, h, g):
+            cols = slice(h * P, (h + 1) * P)
+            nc.vector.quantize_mx(
+                out=codes[side, g][:, cols].bitcast(formats[side]),
+                scales=scales[side, g][:, cols],
+                in_=woven[side, h, g][:].rearrange("p c t -> p (c t)"),
+            )
 
         def multiply(h, g):
             cols = slice(h * P, (h + 1) * P)
             nc.tensor.matmul_mx(
                 out=acc[h][:],
-                lhsT=u_codes[g][:, cols].bitcast(E4M3),
-                lhsT_scale=u_scales[g][:, cols],
-                rhs=g_codes[g][:].bitcast(E5M2),
-                rhs_scale=g_scales[g][:],
+                lhsT=codes["u", g][:, cols].bitcast(E4M3),
+                lhsT_scale=scales["u", g][:, cols],
+                rhs=codes["g", g][:].bitcast(E5M2),
+                rhs_scale=scales["g", g][:],
                 start=(g == 0),
                 stop=(g == PASSES - 1),
             )
@@ -151,63 +157,57 @@ def tile_list_moment_larger_centred_preconditioned_kernel(tc, xf, ra, gt, rb, pc
         def finish(h, tag):
             step = held.tile([P, N], F32, name=f"step{h}", tag=tag, align_bytes=64)
             row = held.tile([P, 1], F32, name=f"row{h}")
-            nc.vector.scalar_tensor_tensor(step[:], acc[h][:], -1.0, pc_sb[:, h, :], ALU.mult, ALU.mult, accum_out=row[:])
-            picked[f"step{h}"] = step
-            picked[f"row{h}"] = row
-
-        def store(h):
-            cols = slice(h * P, (h + 1) * P)
-            step = picked[f"step{h}"]
-            row = picked[f"row{h}"]
+            nc.vector.scalar_tensor_tensor(
+                step[:], acc[h][:], -1.0, pc_sb[:, h, :], ALU.mult, ALU.mult, accum_out=row[:]
+            )
             back = held.tile([P, 1], F32, name=f"back{h}")
             nc.vector.tensor_scalar(back[:], row[:], -0.2 / N, None, ALU.mult)
             new = held.tile([P, N], F32, name=f"new{h}")
             nc.vector.scalar_tensor_tensor(new[:], step[:], back[:], old_sb[:, h, :], ALU.add, ALU.add)
-            nc.sync.dma_start(out[cols, :], new[:])
+            nc.sync.dma_start(out[h * P : (h + 1) * P, :], new[:])
 
-        half = PASS // 2
-        gather("b00", x_rows[0], list_b, 0, True)
-        gather("b01", x_rows[0], list_b, 1, True)
-        gather("b11", x_rows[1], list_b, 1, True, 0, half)
-        gather("a00", x_rows[0], list_a, 0, False)
-        gather("a01", x_rows[0], list_a, 1, False)
-        for h in range(2):
-            for g in range(PASSES):
-                gather(f"g{h}{g}", g_rows[h], list_g, g, False)
-        gather("a10", x_rows[1], list_a, 0, False)
-        gather("b10", x_rows[1], list_b, 0, False)
-        gather("a11", x_rows[1], list_a, 1, False)
-        gather("b11", x_rows[1], list_b, 1, False, half, half)
+        gather("b", 0, 0, True)
+        gather("b", 0, 1, True)
+        gather("g", 0, 1, True, first=GRADIENT_ON_SCALAR)
+        gather("b", 1, 1, True, end=FEATURE_ON_VECTOR)
+        gather("a", 0, 0, False)
+        gather("a", 0, 1, False)
+        gather("g", 0, 0, False)
+        gather("g", 0, 1, False, end=GRADIENT_ON_SCALAR)
+        gather("g", 1, 0, False)
+        gather("g", 1, 1, False)
+        gather("a", 1, 0, False)
+        gather("b", 1, 0, False)
+        gather("a", 1, 1, False)
+        gather("b", 1, 1, False, first=FEATURE_ON_VECTOR)
 
-        larger(0, 0)
-        larger(0, 1)
-        centre(0, 0)
-        centre(0, 1)
-        weigh("wu00", banks["u00"], ra_t, 0)
-        weigh("wu01", banks["u01"], ra_t, 1)
-        centre(1, 0)
         for g in range(PASSES):
-            quantise(f"wu0{g}", u_codes[g], u_scales[g], 0, E4M3)
-        centre(1, 1)
-        weigh("wg00", banks["g00"], rb_t, 0)
-        weigh("wg01", banks["g01"], rb_t, 1)
+            larger(0, g)
+        for g in range(PASSES):
+            centre(0, g)
+        for g in range(PASSES):
+            weigh("u", 0, g)
+        for g in range(PASSES):
+            quantise("u", 0, g)
+        for g in range(PASSES):
+            centre(1, g)
+        for g in range(PASSES):
+            weigh("g", 0, g)
         larger(1, 0)
+        weigh("g", 1, 0)
         for g in range(PASSES):
-            quantise(f"wg0{g}", g_codes[g], g_scales[g], 0, E5M2)
-        larger(1, 1, pieces=2)
-        weigh("wg10", banks["g10"], rb_t, 0)
-        weigh("wg11", banks["g11"], rb_t, 1)
-        weigh("wu10", banks["u10"], ra_t, 0)
+            quantise("g", 0, g)
+        larger(1, 1, cuts=(0, FEATURE_ON_VECTOR, PASS))
+        weigh("g", 1, 1)
+        weigh("u", 1, 0)
         for g in range(PASSES):
-            quantise(f"wg1{g}", g_codes[g], g_scales[g], 1, E5M2)
-        quantise("wu10", u_codes[0], u_scales[0], 1, E4M3)
+            quantise("g", 1, g)
+        quantise("u", 1, 0)
         multiply(0, 0)
         multiply(0, 1)
         multiply(1, 0)
-        weigh("wu11", banks["u11"], ra_t, 1)
-        quantise("wu11", u_codes[1], u_scales[1], 1, E4M3)
+        weigh("u", 1, 1)
+        quantise("u", 1, 1)
         multiply(1, 1)
-        finish(0, "wu11")
-        store(0)
-        finish(1, "step1")
-        store(1)
+        finish(0, tag="woven_u11")
+        finish(1, tag="step1")

from contextlib import ExitStack

import concourse.mybir as mybir
from concourse.masks import make_identity

K, J, N, T = 256, 1024, 256, 2048
P = 128
HALVES = 2
PACK = 4
PASS = P * PACK
PASSES = J // PASS
SET = 8
PER_COLUMN = 16
WEIGHT_ROW = 8
GRADIENT_ON_SCALAR = 256
FEATURE_ON_VECTOR = 384
FLOPS = 2 * K * J * N

F32 = mybir.dt.float32
BF16 = mybir.dt.bfloat16
U32 = mybir.dt.uint32
U16 = mybir.dt.uint16
U8 = mybir.dt.uint8
E4M3 = mybir.dt.float8_e4m3fn_x4
E5M2 = mybir.dt.float8_e5m2_x4
ALU = mybir.AluOpType
COPY = mybir.ActivationFunctionType.Copy


def tile_list_moment_larger_centred_preconditioned_kernel(tc, xf, ra, gt, rb, pc1, old, offs, offs2, offs3, out):
    nc = tc.nc
    with ExitStack() as ctx:
        held = ctx.enter_context(tc.tile_pool(name="held", bufs=1))
        turn = ctx.enter_context(tc.psum_pool(name="turn", bufs=6))
        sums = ctx.enter_context(tc.psum_pool(name="sums", bufs=1))

        lists = {side: held.tile([P, J // PER_COLUMN], U16, name=f"list_{side}") for side in "abg"}
        x_rows = [held.tile([P, T], F32, name=f"x_rows{h}") for h in range(HALVES)]
        g_rows = [held.tile([P, T], F32, name=f"g_rows{h}") for h in range(HALVES)]
        tables = {"a": x_rows, "b": x_rows, "g": g_rows}
        weights = {side: held.tile([P, PASSES, WEIGHT_ROW], F32, name=f"weights_{side}") for side in "ug"}
        pc_sb = held.tile([P, HALVES, N], F32, name="pc_sb")
        old_sb = held.tile([P, HALVES, N], F32, name="old_sb")
        ident = held.tile([P, P], F32, name="ident")

        by_slot = "(g p t) -> p g t"
        nc.sync.dma_start(x_rows[0][:], xf[0:P, :])
        nc.sync.dma_start(lists["a"][:], offs)
        nc.sync.dma_start(lists["b"][:], offs2)
        nc.sync.dma_start(lists["g"][:], offs3)
        nc.sync.dma_start(g_rows[0][:], gt[0:P, :])
        nc.sync.dma_start(g_rows[1][:], gt[P : 2 * P, :])
        nc.sync.dma_start(weights["u"][:, :, 0:PACK], ra[0, :].rearrange(by_slot, p=P, t=PACK))
        nc.sync.dma_start(x_rows[1][:], xf[P : 2 * P, :])
        nc.sync.dma_start(weights["g"][:, :, 0:PACK], rb[0, :].rearrange(by_slot, p=P, t=PACK))
        nc.sync.dma_start(pc_sb[:], pc1.rearrange("(h p) n -> p h n", p=P))
        nc.sync.dma_start(old_sb[:], old.rearrange("(h p) n -> p h n", p=P))

        nc.vector.memset(ident[:], 0.0)
        warm = held.tile([P, 1], F32, name="warm")
        nc.scalar.activation(warm[:], ident[:, 0:1], COPY)
        make_identity(nc, ident[:], nomemset=True)

        codes, scales = {}, {}
        for side, width in (("u", K), ("g", N)):
            for g in range(PASSES):
                codes[side, g] = held.tile([P, width], U32, name=f"codes_{side}{g}", align_bytes=64)
            for g in range(PASSES):
                scales[side, g] = held.tile([P, width], U8, name=f"scales_{side}{g}", align_bytes=64)
        formats = {"u": E4M3, "g": E5M2}
        acc = [sums.tile([P, N], F32, name=f"acc{h}") for h in range(HALVES)]

        picked, banks, woven = {}, {}, {}

        def gather(side, h, g, on_vector, first=0, end=PASS):
            if (side, h, g) not in picked:
                picked[side, h, g] = held.tile([P, PASS], F32, name=f"picked_{side}{h}{g}")
            columns = slice((g * PASS + first) // PER_COLUMN, (g * PASS + end) // PER_COLUMN)
            window = tables[side][h][:].indirect(lists[side][:, columns])
            if on_vector:
                nc.vector.tensor_copy(picked[side, h, g][:, first:end], window)
            else:
                nc.scalar.activation(picked[side, h, g][:, first:end], window, COPY)

        def larger(h, g, cuts=(0, PASS)):
            big = held.tile([P, PACK, P], F32, name=f"big{h}{g}")
            for first, end in zip(cuts, cuts[1:]):
                part = slice(first // PACK, end // PACK)
                nc.vector.tensor_tensor(
                    big[:].rearrange("p t q -> p q t")[:, part, :],
                    picked["a", h, g][:].rearrange("p (q t) -> p q t", t=PACK)[:, part, :],
                    picked["b", h, g][:].rearrange("p (q t) -> p q t", t=PACK)[:, part, :],
                    ALU.max,
                )
            bank = turn.tile([P, PACK, P], F32, name="bank")
            for t in range(PACK):
                nc.tensor.transpose(bank[:, t, :], big[:, t, :], ident[:])
            banks["u", h, g] = bank

        def centre(h, g):
            dense = picked["g", h, g]
            total = held.tile([P, PASS // SET, 1], F32, name=f"total{h}{g}")
            nc.vector.tensor_reduce(
                total[:, :, 0], dense[:].rearrange("p (c i) -> p c i", i=SET), mybir.AxisListType.X, ALU.add
            )
            less = held.tile([P, PASS // SET, SET // PACK], F32, name=f"less{h}{g}")
            nc.gpsimd.tensor_scalar(
                less[:], total[:].to_broadcast([P, PASS // SET, SET // PACK]), -1.0 / SET, 0.0, ALU.mult, ALU.add
            )
            bank = turn.tile([P, PACK, P], F32, name="bank")
            for t in range(PACK):
                nc.tensor.matmul(
                    bank[:, t, :], dense[:, t:PASS:PACK], ident[:], start=(t == 0), stop=False, is_transpose=True
                )
            for t in range(PACK):
                nc.tensor.matmul(
                    bank[:, t, :],
                    less[:].rearrange("p c s -> p (c s)"),
                    ident[:],
                    start=False,
                    stop=(t == PACK - 1),
                    is_transpose=True,
                )
            banks["g", h, g] = bank

        def weigh(side, h, g):
            woven[side, h, g] = held.tile(
                [P, P, PACK], BF16, name=f"woven_{side}{h}{g}", tag=f"woven_{side}{h}{g}", align_bytes=64
            )
            nc.vector.tensor_tensor(
                woven[side, h, g][:],
                banks[side, h, g][:].rearrange("p t c -> p c t"),
                weights[side][:, g : g + 1, 0:PACK].to_broadcast([P, P, PACK]),
                ALU.mult,
            )

        def quantise(side, h, g):
            cols = slice(h * P, (h + 1) * P)
            nc.vector.quantize_mx(
                out=codes[side, g][:, cols].bitcast(formats[side]),
                scales=scales[side, g][:, cols],
                in_=woven[side, h, g][:].rearrange("p c t -> p (c t)"),
            )

        def multiply(h, g):
            cols = slice(h * P, (h + 1) * P)
            nc.tensor.matmul_mx(
                out=acc[h][:],
                lhsT=codes["u", g][:, cols].bitcast(E4M3),
                lhsT_scale=scales["u", g][:, cols],
                rhs=codes["g", g][:].bitcast(E5M2),
                rhs_scale=scales["g", g][:],
                start=(g == 0),
                stop=(g == PASSES - 1),
            )

        def finish(h, tag):
            step = held.tile([P, N], F32, name=f"step{h}", tag=tag, align_bytes=64)
            row = held.tile([P, 1], F32, name=f"row{h}")
            nc.vector.scalar_tensor_tensor(
                step[:], acc[h][:], -1.0, pc_sb[:, h, :], ALU.mult, ALU.mult, accum_out=row[:]
            )
            back = held.tile([P, 1], F32, name=f"back{h}")
            nc.vector.tensor_scalar(back[:], row[:], -0.2 / N, None, ALU.mult)
            new = held.tile([P, N], F32, name=f"new{h}")
            nc.vector.scalar_tensor_tensor(new[:], step[:], back[:], old_sb[:, h, :], ALU.add, ALU.add)
            nc.sync.dma_start(out[h * P : (h + 1) * P, :], new[:])

        gather("b", 0, 0, True)
        gather("b", 0, 1, True)
        gather("g", 0, 1, True, first=GRADIENT_ON_SCALAR)
        gather("b", 1, 1, True, end=FEATURE_ON_VECTOR)
        gather("a", 0, 0, False)
        gather("a", 0, 1, False)
        gather("g", 0, 0, False)
        gather("g", 0, 1, False, end=GRADIENT_ON_SCALAR)
        gather("g", 1, 0, False)
        gather("g", 1, 1, False)
        gather("a", 1, 0, False)
        gather("b", 1, 0, False)
        gather("a", 1, 1, False)
        gather("b", 1, 1, False, first=FEATURE_ON_VECTOR)

        for g in range(PASSES):
            larger(0, g)
        for g in range(PASSES):
            centre(0, g)
        for g in range(PASSES):
            weigh("u", 0, g)
        for g in range(PASSES):
            quantise("u", 0, g)
        for g in range(PASSES):
            centre(1, g)
        for g in range(PASSES):
            weigh("g", 0, g)
        larger(1, 0)
        weigh("g", 1, 0)
        for g in range(PASSES):
            quantise("g", 0, g)
        larger(1, 1, cuts=(0, FEATURE_ON_VECTOR, PASS))
        weigh("g", 1, 1)
        weigh("u", 1, 0)
        for g in range(PASSES):
            quantise("g", 1, g)
        quantise("u", 1, 0)
        multiply(0, 0)
        multiply(0, 1)
        multiply(1, 0)
        weigh("u", 1, 1)
        quantise("u", 1, 1)
        multiply(1, 1)
        finish(0, tag="woven_u11")
        finish(1, tag="step1")
